import numpy as np, ml_dtypes
CORES = [2,6,10,14]
N = 4
def setup_inputs(rng):
    return {"x": rng.standard_normal((N, 128, 256), dtype=np.float32).astype(ml_dtypes.bfloat16)}
def reference(x):
    b = 256 // N
    blocks = x.reshape(N, 128, N, b)
    return {"y": np.ascontiguousarray(blocks.transpose(2, 1, 0, 3)).reshape(N, 128, 256)}

@@ -1,0 +1,40 @@
+from concourse.bass import DstId, RemoteDMATransfer
+
+SCRATCH = {
+    "xs": ("sbuf", [128, 256], "bfloat16"),
+    "land": ("sbuf", [128, 256], "bfloat16"),
+}
+SEMAPHORES = ["loaded", "arrived", "sent", "stored"]
+
+
+def rank_program(g, core, T, topo):
+    r = T.rank_of(core)
+    if r is None:
+        return
+    n = len(T.cores)
+    b = 256 // n
+    sem = T.sem
+
+    def blk(t, j):
+        return t[:, j * b:(j + 1) * b]
+
+    g.sync.dma_start(T.xs[:], T.x[:]).then_inc(sem.loaded, 16)
+    g.sync.dma_start(blk(T.land, r), blk(T.x, r)).then_inc(sem.arrived, 16)
+
+    off_masks = [0x000F, 0x00F0]
+    transfers = []
+    for j in range(n):
+        if j == r:
+            continue
+        dst = T.cores[j]
+        rid, pid, _se = topo.addr(dst)
+        m = 0xFF00 if topo.chip(dst) == topo.chip(core) else off_masks.pop(0)
+        transfers.append(RemoteDMATransfer(dst_ids=[DstId(rid=rid, pnc=pid)], dma_engine_mask=m,
+                                           remote_sem=sem.arrived, src=blk(T.xs, j), dst=blk(T.land, r)))
+    g.wait_ge(sem.loaded, 16)
+    g.remote_dma_fused(transfers, local_sem=sem.sent)
+
+    g.sync.wait_ge(sem.arrived, 32)
+    g.sync.dma_start(T.y[:], T.land[:]).then_inc(sem.stored, 16)
+    g.sync.wait_ge(sem.stored, 16)
+    g.wait_ge(sem.sent, 16)

@@ -1,8 +1,8 @@
 from concourse.bass import DstId, RemoteDMATransfer
 
 SCRATCH = {
-    "xs": ("sbuf", [128, 256], "bfloat16"),
-    "land": ("sbuf", [128, 256], "bfloat16"),
+    "sd": ("dram", [4, 128, 64], "bfloat16"),
+    "ld": ("dram", [4, 128, 64], "bfloat16"),
 }
 SEMAPHORES = ["loaded", "arrived", "sent", "stored"]
 
@@ -18,23 +18,27 @@ def rank_program(g, core, T, topo):
     def blk(t, j):
         return t[:, j * b:(j + 1) * b]
 
-    g.sync.dma_start(T.xs[:], T.x[:]).then_inc(sem.loaded, 16)
-    g.sync.dma_start(blk(T.land, r), blk(T.x, r)).then_inc(sem.arrived, 16)
+    off = [j for j in range(n) if topo.chip(T.cores[j]) != topo.chip(core)]
+    on = [j for j in range(n) if j != r and topo.chip(T.cores[j]) == topo.chip(core)]
+    order = off + on
+    queues = [g.sync, g.scalar, g.sync]
 
-    off_masks = [0x000F, 0x00F0]
+    for q, j in zip(queues, order):
+        q.dma_start(T.sd[j], blk(T.x, j)).then_inc(sem.loaded, 16)
+    g.scalar.dma_start(blk(T.y, r), blk(T.x, r)).then_inc(sem.stored, 16)
+
+    masks = [0x000F, 0x00F0, 0xFF00]
     transfers = []
-    for j in range(n):
-        if j == r:
-            continue
-        dst = T.cores[j]
-        rid, pid, _se = topo.addr(dst)
-        m = 0xFF00 if topo.chip(dst) == topo.chip(core) else off_masks.pop(0)
+    for m, j in zip(masks, order):
+        rid, pid, _se = topo.addr(T.cores[j])
         transfers.append(RemoteDMATransfer(dst_ids=[DstId(rid=rid, pnc=pid)], dma_engine_mask=m,
-                                           remote_sem=sem.arrived, src=blk(T.xs, j), dst=blk(T.land, r)))
-    g.wait_ge(sem.loaded, 16)
+                                           remote_sem=sem.arrived, src=T.sd[j], dst=T.ld[r]))
+    g.wait_ge(sem.loaded, 48)
     g.remote_dma_fused(transfers, local_sem=sem.sent)
 
-    g.sync.wait_ge(sem.arrived, 32)
-    g.sync.dma_start(T.y[:], T.land[:]).then_inc(sem.stored, 16)
-    g.sync.wait_ge(sem.stored, 16)
+    g.sync.wait_ge(sem.arrived, 16)
+    g.scalar.wait_ge(sem.arrived, 16)
+    for q, j in zip(queues, order):
+        q.dma_start(blk(T.y, j), T.ld[j]).then_inc(sem.stored, 16)
+    g.sync.wait_ge(sem.stored, 64)
     g.wait_ge(sem.sent, 16)

@@ -4,7 +4,7 @@ SCRATCH = {
     "sd": ("dram", [4, 128, 64], "bfloat16"),
     "ld": ("dram", [4, 128, 64], "bfloat16"),
 }
-SEMAPHORES = ["loaded", "arrived", "sent", "stored"]
+SEMAPHORES = ["loaded", "arr_on", "arr_off", "sent", "stored"]
 
 
 def rank_program(g, core, T, topo):
@@ -19,26 +19,26 @@ def rank_program(g, core, T, topo):
         return t[:, j * b:(j + 1) * b]
 
     off = [j for j in range(n) if topo.chip(T.cores[j]) != topo.chip(core)]
-    on = [j for j in range(n) if j != r and topo.chip(T.cores[j]) == topo.chip(core)]
-    order = off + on
-    queues = [g.sync, g.scalar, g.sync]
+    on = [j for j in range(n) if j != r and topo.chip(T.cores[j]) == topo.chip(core)][0]
 
-    for q, j in zip(queues, order):
-        q.dma_start(T.sd[j], blk(T.x, j)).then_inc(sem.loaded, 16)
+    g.sync.dma_start(T.sd[off[0]], blk(T.x, off[0])).then_inc(sem.loaded, 16)
+    g.scalar.dma_start(T.sd[off[1]], blk(T.x, off[1])).then_inc(sem.loaded, 16)
+    g.sync.dma_start(T.sd[on], blk(T.x, on)).then_inc(sem.loaded, 16)
     g.scalar.dma_start(blk(T.y, r), blk(T.x, r)).then_inc(sem.stored, 16)
 
-    masks = [0x000F, 0x00F0, 0xFF00]
     transfers = []
-    for m, j in zip(masks, order):
+    for m, j, s in ((0x000F, off[0], sem.arr_off), (0x00F0, off[1], sem.arr_off), (0xFF00, on, sem.arr_on)):
         rid, pid, _se = topo.addr(T.cores[j])
         transfers.append(RemoteDMATransfer(dst_ids=[DstId(rid=rid, pnc=pid)], dma_engine_mask=m,
-                                           remote_sem=sem.arrived, src=T.sd[j], dst=T.ld[r]))
+                                           remote_sem=s, src=T.sd[j], dst=T.ld[r]))
     g.wait_ge(sem.loaded, 48)
     g.remote_dma_fused(transfers, local_sem=sem.sent)
 
-    g.sync.wait_ge(sem.arrived, 16)
-    g.scalar.wait_ge(sem.arrived, 16)
-    for q, j in zip(queues, order):
-        q.dma_start(blk(T.y, j), T.ld[j]).then_inc(sem.stored, 16)
+    g.sync.wait_ge(sem.arr_on, 8)
+    g.sync.dma_start(blk(T.y, on), T.ld[on]).then_inc(sem.stored, 16)
+    g.sync.wait_ge(sem.arr_off, 8)
+    g.sync.dma_start(blk(T.y, off[0]), T.ld[off[0]]).then_inc(sem.stored, 16)
+    g.scalar.wait_ge(sem.arr_off, 8)
+    g.scalar.dma_start(blk(T.y, off[1]), T.ld[off[1]]).then_inc(sem.stored, 16)
     g.sync.wait_ge(sem.stored, 64)
     g.wait_ge(sem.sent, 16)

@@ -4,7 +4,7 @@ SCRATCH = {
     "sd": ("dram", [4, 128, 64], "bfloat16"),
     "ld": ("dram", [4, 128, 64], "bfloat16"),
 }
-SEMAPHORES = ["loaded", "arr_on", "arr_off", "sent", "stored"]
+SEMAPHORES = ["loaded", "loaded_on", "go", "arr_on", "arr_off", "sent", "stored"]
 
 
 def rank_program(g, core, T, topo):
@@ -18,21 +18,26 @@ def rank_program(g, core, T, topo):
     def blk(t, j):
         return t[:, j * b:(j + 1) * b]
 
+    def tr(m, j, s):
+        rid, pid, _se = topo.addr(T.cores[j])
+        return RemoteDMATransfer(dst_ids=[DstId(rid=rid, pnc=pid)], dma_engine_mask=m,
+                                 remote_sem=s, src=T.sd[j], dst=T.ld[r])
+
     off = [j for j in range(n) if topo.chip(T.cores[j]) != topo.chip(core)]
     on = [j for j in range(n) if j != r and topo.chip(T.cores[j]) == topo.chip(core)][0]
 
     g.sync.dma_start(T.sd[off[0]], blk(T.x, off[0])).then_inc(sem.loaded, 16)
     g.scalar.dma_start(T.sd[off[1]], blk(T.x, off[1])).then_inc(sem.loaded, 16)
-    g.sync.dma_start(T.sd[on], blk(T.x, on)).then_inc(sem.loaded, 16)
-    g.scalar.dma_start(blk(T.y, r), blk(T.x, r)).then_inc(sem.stored, 16)
+    g.sync.dma_start(T.sd[on], blk(T.x, on)).then_inc(sem.loaded_on, 16)
 
-    transfers = []
-    for m, j, s in ((0x000F, off[0], sem.arr_off), (0x00F0, off[1], sem.arr_off), (0xFF00, on, sem.arr_on)):
-        rid, pid, _se = topo.addr(T.cores[j])
-        transfers.append(RemoteDMATransfer(dst_ids=[DstId(rid=rid, pnc=pid)], dma_engine_mask=m,
-                                           remote_sem=s, src=T.sd[j], dst=T.ld[r]))
-    g.wait_ge(sem.loaded, 48)
-    g.remote_dma_fused(transfers, local_sem=sem.sent)
+    g.wait_ge(sem.loaded, 32)
+    g.remote_dma_fused([tr(0x000F, off[0], sem.arr_off), tr(0x00F0, off[1], sem.arr_off)], local_sem=sem.sent)
+    g.sem_inc(sem.go, 1)
+    g.wait_ge(sem.loaded_on, 16)
+    g.remote_dma_fused([tr(0xFF00, on, sem.arr_on)], local_sem=sem.sent)
+
+    g.scalar.wait_ge(sem.go, 1)
+    g.scalar.dma_start(blk(T.y, r), blk(T.x, r)).then_inc(sem.stored, 16)
 
     g.sync.wait_ge(sem.arr_on, 8)
     g.sync.dma_start(blk(T.y, on), T.ld[on]).then_inc(sem.stored, 16)

@@ -4,7 +4,7 @@ SCRATCH = {
     "sd": ("dram", [4, 128, 64], "bfloat16"),
     "ld": ("dram", [4, 128, 64], "bfloat16"),
 }
-SEMAPHORES = ["loaded", "loaded_on", "go", "arr_on", "arr_off", "sent", "stored"]
+SEMAPHORES = ["ld1", "ld2", "ld3", "go", "arr1", "arr2", "arr3", "sent", "stored"]
 
 
 def rank_program(g, core, T, topo):
@@ -18,32 +18,32 @@ def rank_program(g, core, T, topo):
     def blk(t, j):
         return t[:, j * b:(j + 1) * b]
 
-    def tr(m, j, s):
+    def send(m, j, s):
         rid, pid, _se = topo.addr(T.cores[j])
-        return RemoteDMATransfer(dst_ids=[DstId(rid=rid, pnc=pid)], dma_engine_mask=m,
-                                 remote_sem=s, src=T.sd[j], dst=T.ld[r])
+        g.remote_dma(T.ld[r], T.sd[j], s, sem.sent, pid, rid, m)
 
-    off = [j for j in range(n) if topo.chip(T.cores[j]) != topo.chip(core)]
-    on = [j for j in range(n) if j != r and topo.chip(T.cores[j]) == topo.chip(core)][0]
+    p1, p2, p3 = r ^ 2, r ^ 3, r ^ 1
 
-    g.sync.dma_start(T.sd[off[0]], blk(T.x, off[0])).then_inc(sem.loaded, 16)
-    g.scalar.dma_start(T.sd[off[1]], blk(T.x, off[1])).then_inc(sem.loaded, 16)
-    g.sync.dma_start(T.sd[on], blk(T.x, on)).then_inc(sem.loaded_on, 16)
+    g.sync.dma_start(T.sd[p1], blk(T.x, p1)).then_inc(sem.ld1, 16)
+    g.sync.dma_start(T.sd[p2], blk(T.x, p2)).then_inc(sem.ld2, 16)
+    g.sync.dma_start(T.sd[p3], blk(T.x, p3)).then_inc(sem.ld3, 16)
 
-    g.wait_ge(sem.loaded, 32)
-    g.remote_dma_fused([tr(0x000F, off[0], sem.arr_off), tr(0x00F0, off[1], sem.arr_off)], local_sem=sem.sent)
+    g.wait_ge(sem.ld1, 16)
+    send(0x00FF, p1, sem.arr1)
+    g.wait_ge(sem.ld2, 16)
+    send(0x00FF, p2, sem.arr2)
     g.sem_inc(sem.go, 1)
-    g.wait_ge(sem.loaded_on, 16)
-    g.remote_dma_fused([tr(0xFF00, on, sem.arr_on)], local_sem=sem.sent)
+    g.wait_ge(sem.ld3, 16)
+    send(0xFF00, p3, sem.arr3)
 
     g.scalar.wait_ge(sem.go, 1)
     g.scalar.dma_start(blk(T.y, r), blk(T.x, r)).then_inc(sem.stored, 16)
 
-    g.sync.wait_ge(sem.arr_on, 8)
-    g.sync.dma_start(blk(T.y, on), T.ld[on]).then_inc(sem.stored, 16)
-    g.sync.wait_ge(sem.arr_off, 8)
-    g.sync.dma_start(blk(T.y, off[0]), T.ld[off[0]]).then_inc(sem.stored, 16)
-    g.scalar.wait_ge(sem.arr_off, 8)
-    g.scalar.dma_start(blk(T.y, off[1]), T.ld[off[1]]).then_inc(sem.stored, 16)
+    g.sync.wait_ge(sem.arr1, 8)
+    g.sync.dma_start(blk(T.y, p1), T.ld[p1]).then_inc(sem.stored, 16)
+    g.sync.wait_ge(sem.arr3, 8)
+    g.sync.dma_start(blk(T.y, p3), T.ld[p3]).then_inc(sem.stored, 16)
+    g.scalar.wait_ge(sem.arr2, 8)
+    g.scalar.dma_start(blk(T.y, p2), T.ld[p2]).then_inc(sem.stored, 16)
     g.sync.wait_ge(sem.stored, 64)
-    g.wait_ge(sem.sent, 16)
+    g.wait_ge(sem.sent, 24)

from concourse.bass import DstId, RemoteDMATransfer

SCRATCH = {
    "sd": ("dram", [4, 128, 64], "bfloat16"),
    "ld": ("dram", [4, 128, 64], "bfloat16"),
}
SEMAPHORES = ["ld1", "ld2", "ld3", "go", "arr1", "arr2", "arr3", "sent", "stored"]


def rank_program(g, core, T, topo):
    r = T.rank_of(core)
    if r is None:
        return
    n = len(T.cores)
    b = 256 // n
    sem = T.sem

    def blk(t, j):
        return t[:, j * b:(j + 1) * b]

    def send(m, j, s):
        rid, pid, _se = topo.addr(T.cores[j])
        g.remote_dma(T.ld[r], T.sd[j], s, sem.sent, pid, rid, m)

    p1, p2, p3 = r ^ 2, r ^ 3, r ^ 1

    g.sync.dma_start(T.sd[p1], blk(T.x, p1)).then_inc(sem.ld1, 16)
    g.sync.dma_start(T.sd[p2], blk(T.x, p2)).then_inc(sem.ld2, 16)
    g.sync.dma_start(T.sd[p3], blk(T.x, p3)).then_inc(sem.ld3, 16)

    g.wait_ge(sem.ld1, 16)
    send(0x00FF, p1, sem.arr1)
    g.wait_ge(sem.ld2, 16)
    send(0x00FF, p2, sem.arr2)
    g.sem_inc(sem.go, 1)
    g.wait_ge(sem.ld3, 16)
    send(0xFF00, p3, sem.arr3)

    g.scalar.wait_ge(sem.go, 1)
    g.scalar.dma_start(blk(T.y, r), blk(T.x, r)).then_inc(sem.stored, 16)

    g.sync.wait_ge(sem.arr1, 8)
    g.sync.dma_start(blk(T.y, p1), T.ld[p1]).then_inc(sem.stored, 16)
    g.sync.wait_ge(sem.arr3, 8)
    g.sync.dma_start(blk(T.y, p3), T.ld[p3]).then_inc(sem.stored, 16)
    g.scalar.wait_ge(sem.arr2, 8)
    g.scalar.dma_start(blk(T.y, p2), T.ld[p2]).then_inc(sem.stored, 16)
    g.sync.wait_ge(sem.stored, 64)
    g.wait_ge(sem.sent, 24)
